import numpy as np, ml_dtypes
CORES = [40,64,80,88,96,104,120,144]
N = 8
BF = ml_dtypes.bfloat16
def f(rng, *shape):
    return (rng.standard_normal(shape, dtype=np.float32) * np.exp2(rng.integers(-2, 3, shape[:-1] + (1,)))).astype(BF)
def wide(rng, *shape):
    v = f(rng, *shape).astype(np.float32); k = shape[:-2] + (1, shape[-1])
    return (v * np.exp2(rng.integers(-6, 7, k)) * (rng.random(k) > 0.0625)).astype(BF)
def gentries(a):
    return np.ascontiguousarray(a.reshape(8, 16, -1).transpose(0, 2, 1)).reshape(8, -1)
def gtable(e):
    e = np.asarray(e); return np.ascontiguousarray(e.reshape(8, -1, 16).transpose(0, 2, 1)).reshape(128, -1).astype(np.int32)
B, M, W, S = 256, 16, 128, 1280
WL, WM, CB, CW = 1, 8, 24, 112
D, FR = 256, 1
MB = M // 16
U, UB = CW // MB, S // MB
def book(rng, v):
    return (v.astype(np.float32) * (1 + rng.random(v.shape, dtype=np.float32))).astype(np.float32)
def parts(rng, k, s, exact):
    v = rng.integers(WL, WM + 1, k); t = s if exact else min(s, int(np.sum(v)))
    while np.sum(v) != t:
        e = 1 if np.sum(v) < t else -1
        i = np.flatnonzero(v < WM) if e > 0 else np.flatnonzero(v > WL)
        v[rng.permutation(i)[:abs(t - int(np.sum(v)))]] += e
    return v
def widths(rng):
    w = np.zeros((N, 8, B), np.int64)
    for q in range(N):
        for g in range(8):
            w[q, g] = parts(rng, B, UB, False); w[q, g, rng.integers(B)] = WL
    return w
def pick(rng, w, c, cand):
    left = U; lo = int(np.min(w[cand])); out = []
    for i in range(c):
        ok = cand[w[cand] <= left - (c - 1 - i) * lo]
        b = int(ok[rng.integers(len(ok))]); out.append(b); left -= int(w[b])
    return out
def wants(rng, w, uneven=False, full=None):
    L = np.zeros((N, 8, W), np.int64)
    for r in range(N):
        for g in range(8):
            q0 = -1
            own = np.repeat(rng.permutation(N), CB)
            if not uneven: own = rng.permutation(own)
            if full is not None:
                q0 = (r + 1 + g % (N - 1)) % N
                own = np.concatenate([np.full(CB, q0), own[own != q0]])
            c = np.bincount(own[:W], minlength=N); e = []
            for q in range(N):
                if q == q0:
                    e += [q * B + int(b) for b in full[q, g]]
                elif c[q]:
                    cand = np.arange(B)
                    if uneven and rng.random() < 0.5: cand = np.array([int(np.argmin(w[q, g])), int(rng.integers(B))])
                    e += [q * B + b for b in pick(rng, w[q, g], int(c[q]), cand)]
            L[r, g] = rng.permutation(np.array(e))
    return L
def make(rng, w, L, s):
    return {"strm": s.astype(np.int32), "wd": np.stack([gtable(u) for u in w]), "want": np.stack([gtable(u) for u in L]), "dic": book(rng, f(rng, N, 8 * FR, D))}
def setup_inputs(rng):
    w = widths(rng)
    return make(rng, w, wants(rng, w), rng.integers(0, 65536, (N, 8, S)))
def setup_inputs_full(rng):
    w = np.zeros((N, 8, B), np.int64); full = np.zeros((N, 8, CB), np.int64)
    for q in range(N):
        for g in range(8):
            p = np.concatenate([np.array([0, B - 1]), rng.permutation(np.arange(1, B - 1))])
            w[q, g, p[:CB]] = parts(rng, CB, U, True); w[q, g, p[CB:]] = parts(rng, B - CB, UB - U, True); full[q, g] = p[:CB]
    return make(rng, w, wants(rng, w, full=full), rng.integers(0, 65536, (N, 8, S)))
def setup_inputs_uneven(rng):
    w = widths(rng)
    return make(rng, w, wants(rng, w, uneven=True), rng.integers(0, 65536, (N, 8, S)))
def setup_inputs_ends(rng):
    w = np.full((N, 8, B), WL, np.int64); most = min(B - 1, (UB - B * WL) // (WM - WL))
    for q in range(N):
        for g in range(8):
            w[q, g, rng.permutation(B)[:rng.integers(0, most + 1)]] = WM
    s = rng.choice(np.array([0, 0, 1, 32768, 65535, 65535]), (N, 8, S))
    s = np.where(rng.random((N, 8, S)) < 0.25, rng.integers(0, 65536, (N, 8, S)), s)
    return make(rng, w, wants(rng, w), s)
def setup_inputs_spread(rng):
    d = setup_inputs(rng); d["dic"] = book(rng, wide(rng, N, 8 * FR, D)); return d
def check_inputs(d):
    try:
        bad = []
        if d["strm"].min() < 0 or d["strm"].max() > 65535: bad.append("words")
        if not np.isfinite(d["dic"].astype(np.float32)).all(): bad.append("finite")
        w = np.stack([gentries(u) for u in d["wd"]]).astype(np.int64); L = np.stack([gentries(u) for u in d["want"]]).astype(np.int64)
        if w.min() < WL or w.max() > WM: bad.append("widths")
        if (MB * np.sum(w, axis=2) > S).any(): bad.append("words of a column")
        if L.min() < 0 or L.max() >= N * B: return bad + ["wanted blocks"]
        n = np.zeros((N, 8, N), np.int64); m = np.zeros((N, 8, N), np.int64)
        for r in range(N):
            for g in range(8):
                q, b = L[r, g] // B, L[r, g] % B
                np.add.at(n[r, g], q, 1); np.add.at(m[r, g], q, MB * w[q, g, b])
        if n.max() > CB: bad.append("blocks of a pair")
        if m.max() > CW: bad.append("words of a pair")
        return bad
    except Exception:
        return ["shapes"]
def reference(strm, wd, want, dic):
    y = np.zeros((N, 8 * FR, W * M), dic.dtype)
    bit = (strm.astype(np.int64)[..., None] >> np.arange(16) & 1).reshape(N, 8, 16 * S)
    w = np.stack([gentries(wd[q]) for q in range(N)]).astype(np.int64)
    first = M * (np.add.accumulate(w, axis=2) - w)
    for r in range(N):
        L = gentries(want[r]).astype(np.int64)
        for g in range(8):
            q, b = L[g] // B, L[g] % B
            v = w[q, g, b][:, None]; at = first[q, g, b][:, None] + np.arange(M) * v
            code = np.zeros((W, M), np.int64)
            for k in range(WM):
                code += np.where(k < v, bit[q[:, None], g, np.minimum(at + k, 16 * S - 1)], 0) << k
            y[r, FR * g:FR * (g + 1)] = dic[r, FR * g:FR * (g + 1)][:, code.reshape(-1)]
    return {"y": y}

from concourse.bass import DstId, RemoteDMATransfer
from concourse.mybir import AluOpType as A, ActivationFunctionType as AF

S, B, NB = 1280, 256, 24
Z0, RSP, R0, ZW = 0, 2048, 2304, 2592

SCRATCH = {
    "wn": ("sbuf", [128, S], "int32"),
    "wnt": ("sbuf", [128, 8], "int32"),
    "wdt": ("sbuf", [128, 16], "int32"),
    "dicw": ("sbuf", [128, 256], "float32"),
    "zb": ("sbuf", [128, ZW], "bfloat16"),
    "ip": ("sbuf", [128, 4], "int32"),
    "c16": ("sbuf", [128, 16], "int32"),
    "g16": ("sbuf", [128, 128], "bfloat16"),
    "ia": ("sbuf", [128, 128], "bfloat16"),
    "q2": ("sbuf", [128, 64], "bfloat16"),
    "it": ("sbuf", [128, 160], "float32"),
    "vv": ("sbuf", [128, 64], "float32"),
    "g64": ("sbuf", [128, 64], "float32"),
    "bi": ("sbuf", [128, 8], "int32"),
    "bf": ("sbuf", [128, 8], "float32"),
    "cf": ("sbuf", [128, 8], "float32"),
    "k1": ("sbuf", [128, 4], "uint16"),
    "k5": ("sbuf", [128, 8], "uint16"),
    "k8": ("sbuf", [128, 2], "uint16"),
    "ones": ("sbuf", [128, 128], "bfloat16"),
    "ltri": ("sbuf", [128, 128], "bfloat16"),
    "msk": ("sbuf", [128, 128], "bfloat16"),
    "qv": ("sbuf", [128, 8], "int32"),
    "bv": ("sbuf", [128, 8], "int32"),
    "oh": ("sbuf", [128, 64], "bfloat16"),
    "vm": ("sbuf", [128, 128], "bfloat16"),
    "ev": ("sbuf", [128, 128], "bfloat16"),
    "sc": ("sbuf", [128, 64], "float32"),
    "so": ("sbuf", [128, 8], "uint16"),
    "sl": ("sbuf", [128, 8], "uint16"),
    "tt": ("sbuf", [128, 512], "bfloat16"),
    "rqo": ("sbuf", [128, 16], "uint16"),
    "rqi": ("sbuf", [128, 16], "uint16"),
    "rl1": ("sbuf", [128, 16], "uint16"),
    "rl2": ("sbuf", [128, 64], "bfloat16"),
    "d0": ("sbuf", [128, 144], "float32"),
    "d1": ("sbuf", [128, 144], "float32"),
    "ft": ("sbuf", [128, 144], "bfloat16"),
    "t1": ("sbuf", [128, 64], "float32"),
    "t2": ("sbuf", [128, 64], "float32"),
    "po": ("sbuf", [128, 64], "uint16"),
    "pm": ("sbuf", [128, 1024], "bfloat16"),
    "two": ("sbuf", [128, 16], "float32"),
    "pw": ("sbuf", [128, 16], "float32"),
    "wb": ("sbuf", [128, 16], "bfloat16"),
    "ws": ("sbuf", [128, 16], "bfloat16"),
    "br": ("sbuf", [128, 16], "float32"),
    "wt": ("sbuf", [128, 16], "float32"),
    "su": ("sbuf", [128, 16], "uint16"),
    "wo": ("sbuf", [128, 16], "uint16"),
    "wu": ("sbuf", [128, 16], "uint16"),
    "b1": ("sbuf", [128, 256], "int32"),
    "b2": ("sbuf", [128, 256], "int32"),
    "u1": ("sbuf", [128, 256], "int32"),
    "u2": ("sbuf", [128, 256], "int32"),
    "u3": ("sbuf", [128, 256], "int32"),
    "tab": ("sbuf", [128, 256], "int32"),
    "sx": ("sbuf", [128, 128], "bfloat16"),
    "sd": ("sbuf", [128, 96], "bfloat16"),
    "cu": ("sbuf", [128, 128], "uint16"),
    "yy": ("sbuf", [128, 2048], "float32"),
    "psx": ("psum", [128, 512], "float32"),
    "pse": ("psum", [128, 512], "float32"),
    "pss": ("psum", [128, 512], "float32"),
    "psd": ("psum", [128, 512], "float32"),
}
SEMAPHORES = [
    "want", "wd", "win", "dic", "st0", "st1", "tail", "zh", "zc", "zr", "dz",
    "ip", "c16", "g16", "q2", "ia", "ltri", "gd", "bi", "bf", "ones", "kk", "k8a", "msk",
    "qv", "oh", "bv", "vm", "px", "pe", "ev", "sc", "so", "sl", "rs", "tt", "rqo",
    "cf", "dd", "ft", "t1", "t2", "po", "pm", "two", "pw", "wb", "ws", "ps", "su", "br", "wt", "wo",
    "b1", "b2", "zs", "pd", "u1", "u2", "u3", "tab", "sx", "sd", "own", "cu", "y0", "y1",
    "loc", "h1", "h2", "rqx", "rqd", "rsx", "rsd",
]


def _mask(engines):
    m = 0
    for e in engines:
        m |= 1 << e
    return m


def _deal(engines, k):
    size = 1
    while 2 * size * k <= len(engines):
        size *= 2
    sizes = [size] * k
    i = k - 1
    while i >= 0 and sum(sizes) + size <= len(engines):
        sizes[i] *= 2
        i -= 1
    out, at = [], 0
    for s in sizes:
        out.append(engines[at:at + s])
        at += s
    return out


def _routes(T, topo):
    cores = list(T.cores)
    n = len(cores)
    R = []
    for r in range(n):
        c = cores[r]
        direct = [q for q in range(n) if q != r and topo.may_write(c, cores[q])]
        cross = [q for q in range(n) if q != r and q not in direct]
        able = [h for h in topo.cores_of(c) if h not in cores and all(topo.may_write(h, cores[q]) for q in cross)]
        near = [h for h in able if topo.die(h) == topo.die(c)]
        far = [h for h in able if topo.die(h) != topo.die(c)]
        relays = [near[0], far[0]]
        off = topo.engines(c, cores[direct[0]])
        on = topo.engines(c, relays[0])
        only = [e for e in on if e not in off]
        R.append({"direct": direct, "cross": cross, "relays": relays,
                  "e_dir": _deal(off, len(direct)), "e_r1": _deal(only, 2), "e_r2": _deal(on, 2)})
    return R


def _dst(topo, d, s):
    rid, pid = topo.addr(d, s)
    return DstId(rid=rid, pnc=pid)


def _relay_engines(topo, h, dests):
    return _deal(topo.engines(h, dests[0]), len(dests))


def _relay(g, core, T, topo, R, r, k):
    cores = list(T.cores)
    me = R[r]
    mine = me["cross"][2 * k:2 * k + 2]
    eng = _relay_engines(topo, core, [cores[q] for q in mine])
    g.wait_ge(T.sem.h1, len(me["e_r1"][k]))
    tr = []
    for i, q in enumerate(mine):
        at = 2 * R[q]["cross"].index(r)
        tr.append(RemoteDMATransfer(dst_ids=[_dst(topo, cores[q], core)], dma_engine_mask=_mask(eng[i]),
                                    remote_sem=T.sem.rqx, src=T.rl1[:, 2 * q:2 * q + 2], dst=T.rqi[:, at:at + 2]))
    g.remote_dma_fused(tr, local_sem=T.sem.loc)
    g.wait_ge(T.sem.h2, len(me["e_r2"][k]))
    tr = []
    for i, q in enumerate(mine):
        tr.append(RemoteDMATransfer(dst_ids=[_dst(topo, cores[q], core)], dma_engine_mask=_mask(eng[i]),
                                    remote_sem=T.sem.rsx, src=T.rl2[:, 32 * i:32 * i + NB],
                                    dst=T.zb[:, RSP + 32 * r:RSP + 32 * r + NB]))
    g.remote_dma_fused(tr, local_sem=T.sem.loc)
    g.wait_ge(T.sem.loc, 2 * sum(len(e) for e in eng))


def rank_program(g, core, T, topo):
    R = _routes(T, topo)
    cores = list(T.cores)
    rank = T.rank_of(core)
    if rank is None:
        for r in range(len(cores)):
            if core in R[r]["relays"]:
                _relay(g, core, T, topo, R, r, R[r]["relays"].index(core))
        return
    me = R[rank]
    V, SC, PE, SY = g.vector, g.scalar, g.tensor, g.sync
    Q = {"g": g, "v": V, "s": SC, "p": PE, "y": SY}
    cnt, seen = {}, {}

    def inc(ins, name, n=1):
        ins.then_inc(T.sem[name], n)
        cnt[name] = cnt.get(name, 0) + n

    def need(q, *names):
        for name in names:
            if seen.get((q, name), 0) < cnt[name]:
                Q[q].wait_ge(T.sem[name], cnt[name])
                seen[(q, name)] = cnt[name]

    def ts(name, out, in0, s1, s2, op0, op1=None):
        if op1 is None:
            inc(V.tensor_scalar(out, in0, s1, None, op0), name)
        else:
            inc(V.tensor_scalar(out, in0, s1, s2, op0, op1), name)

    nx = nd = 0
    for q in me["cross"]:
        i = R[q]["cross"].index(rank)
        h = R[q]["relays"][i // 2]
        nx += len(_relay_engines(topo, h, [cores[a] for a in R[q]["cross"][i - i % 2:i - i % 2 + 2]])[i % 2])
    for q in me["direct"]:
        nd += len(R[q]["e_dir"][R[q]["direct"].index(rank)])
    cnt["rqx"] = cnt["rsx"] = nx
    cnt["rqd"] = cnt["rsd"] = nd

    inc(SY.dma_start(T.wnt[:], T.want[:]), "want", 16)
    inc(SC.dma_start(T.wdt[:], T.wd[:]), "wd", 16)
    inc(V.memset(T.wn[:, S - 8:S], 0), "tail")
    inc(V.memset(T.zb[:, 1024:2048], 0.0), "zh")
    need("y", "tail")
    need("s", "tail")
    for m in range(16):
        s = m // 2
        inc((SY if m % 2 == 0 else SC).dma_start(T.wn[m::16, 0:S - s], T.strm[:, s:S]), "win", 16)
    need("s", "zh")
    inc(SC.activation(T.zb[:, 0:1024], T.zb[:, 1024:2048], AF.Copy), "zc")

    inc(g.iota(T.ip[:, 0:1], [[0, 1]], 0, 1), "ip")
    inc(g.iota(T.g16[:], [[16, 8], [0, 16]], 0, 0, allow_small_or_imprecise_dtypes=True), "g16")
    inc(g.iota(T.c16[:], [[16, 16]], 0, 0), "c16")
    inc(g.iota(T.q2[:], [[0, 8], [2, 8]], 0, 0, allow_small_or_imprecise_dtypes=True), "q2")
    p = T.ip[:, 0:1]
    need("v", "ip")
    ts("bi", T.bi[:, 0:1], p, 15, None, A.bitwise_and)
    ts("bi", T.bi[:, 1:2], p, 16, None, A.bitwise_and)
    ts("bi", T.bi[:, 2:3], p, 112, None, A.bitwise_and)
    ts("bi", T.bi[:, 3:4], p, 1, None, A.bitwise_and)
    ts("bi", T.bi[:, 4:5], p, 3, 1, A.logical_shift_right, A.bitwise_and)
    need("v", "bi")
    inc(V.tensor_copy(T.bf[:, 0:5], T.bi[:, 0:5]), "bf")
    pa, par, pb, p1, b3 = (T.bf[:, i:i + 1] for i in range(5))
    need("v", "bf", "g16")
    ts("ones", T.ones[:], T.g16[:], pb, 1.0 / 256, A.is_equal, A.mult)
    need("g", "ones")
    inc(g.affine_select(T.ltri[:], T.ones[:], [[1, 128]], A.is_gt, 0.0, 0, -1), "ltri")
    inc(g.iota(T.ia[:], [[0, 8], [1, 16]], 0, 0, allow_small_or_imprecise_dtypes=True), "ia")
    inc(g.iota(T.it[:], [[1, 160]], -17, 0, allow_small_or_imprecise_dtypes=True), "gd")
    inc(g.iota(T.vv[:], [[1, 8], [0, 8]], 1, 0, allow_small_or_imprecise_dtypes=True), "gd")
    inc(g.iota(T.g64[:], [[0, 8], [16, 8]], 0, 0, allow_small_or_imprecise_dtypes=True), "gd")
    need("v", "c16")
    ts("kk", T.k1[:], T.c16[:, 0:4], 0.125, b3, A.mult, A.add)
    ts("kk", T.k5[:], T.c16[:, 0:8], 0.0625, None, A.mult)
    ts("k8a", T.cf[:, 0:1], pa, 16.0, par, A.mult, A.add)
    inc(V.memset(T.zb[:, RSP:ZW], 0.0), "zr")
    need("v", "k8a")
    ts("kk", T.k8[:, 0:1], p1, 240.0, T.cf[:, 0:1], A.mult, A.add)

    need("p", "ones", "q2")
    PE.matmul(T.psx[:, 0:64], T.ones[:], T.q2[:], True, False)
    need("v", "want")
    ts("qv", T.qv[:], T.wnt[:], 7, 14, A.logical_shift_right, A.bitwise_and)
    ts("bv", T.bv[:], T.wnt[:], 255, None, A.bitwise_and)
    need("v", "kk", "q2", "qv")
    inc(V.tensor_tensor(T.oh[:], T.qv[:].indirect(T.k1[:]), T.q2[:], A.is_equal), "oh")
    need("p", "oh")
    for d in range(1, 8):
        PE.matmul(T.psx[:, 8 * d:64], T.ones[:], T.oh[:, 0:64 - 8 * d], False, False)
    need("p", "ltri")
    inc(PE.matmul(T.psx[:, 0:64], T.ltri[:], T.oh[:], False, True), "px")
    need("v", "ia")
    ts("msk", T.msk[:], T.ia[:], pa, None, A.is_equal)
    need("v", "msk", "bv")
    inc(V.tensor_tensor(T.vm[:], T.bv[:].indirect(T.k5[:]), T.msk[:], A.mult), "vm")
    need("p", "vm")
    inc(PE.matmul(T.pse[:, 0:128], T.ones[:], T.vm[:], True, True), "pe")
    need("s", "pe")
    inc(SC.activation(T.ev[:], T.pse[:, 0:128], AF.Copy, scale=256.0), "ev")
    need("v", "px", "oh")
    inc(V.tensor_tensor_scan(T.sc[:], T.oh[:], T.psx[:, 0:64], 0.0, A.max, A.min), "sc")
    need("v", "sc")
    ts("so", T.so[:], T.sc[:, 7::8], 256.0, par, A.mult, A.add)
    need("v", "so", "zr", "ev")
    inc(V.tensor_copy(T.zb[:, R0:R0 + 272].indirect(T.so[:]), T.ev[:]), "rs")
    need("v", "rs")
    inc(V.transpose(T.tt[:, 0:256], T.zb[:, R0:R0 + 256]), "tt")
    inc(V.transpose(T.tt[:, 256:512], T.zb[:, R0 + 16:R0 + 272]), "tt")
    need("v", "tt")
    inc(V.tensor_copy(T.rqo[:], T.tt[:].indirect(T.k8[:, 0:1])), "rqo")

    nloc = 0
    need("g", "rqo")
    tr = [RemoteDMATransfer(dst_ids=[_dst(topo, h, core)], dma_engine_mask=_mask(me["e_r1"][k]),
                            remote_sem=T.sem.h1, src=T.rqo[:], dst=T.rl1[:]) for k, h in enumerate(me["relays"])]
    g.remote_dma_fused(tr, local_sem=T.sem.loc)
    nloc += sum(len(e) for e in me["e_r1"])
    tr = []
    for i, q in enumerate(me["direct"]):
        at = 8 + 2 * R[q]["direct"].index(rank)
        tr.append(RemoteDMATransfer(dst_ids=[_dst(topo, cores[q], core)], dma_engine_mask=_mask(me["e_dir"][i]),
                                    remote_sem=T.sem.rqd, src=T.rqo[:, 2 * q:2 * q + 2], dst=T.rqi[:, at:at + 2]))
    g.remote_dma_fused(tr, local_sem=T.sem.loc)
    nloc += sum(len(e) for e in me["e_dir"])

    ts("cf", T.cf[:, 1:2], pa, 8.0, None, A.mult)
    ts("cf", T.cf[:, 2:3], pa, 1.0, None, A.add)
    ts("cf", T.cf[:, 3:4], p1, -255.0, 256.0, A.mult, A.add)
    need("v", "wd")
    inc(V.tensor_copy(T.wb[:], T.wdt[:]), "wb")
    need("v", "cf", "gd")
    ts("dd", T.d0[:], T.it[:, 0:144], T.cf[:, 1:2], 0.5, A.not_equal, A.mult)
    ts("dd", T.d1[:], T.it[:, 16:160], T.cf[:, 1:2], 32768.0, A.is_equal, A.mult)
    ts("t1", T.t1[:], T.g64[:], pb, T.cf[:, 2:3], A.is_equal, A.mult)
    need("v", "wb")
    inc(V.tensor_tensor_scan(T.ws[:, 1:16], T.wb[:, 0:15], T.wb[:, 0:15], 0.0, A.add, A.max), "ws")
    need("p", "wb")
    PE.matmul(T.pss[:, 0:16], T.ltri[:], T.wb[:], True, False)
    need("p", "ws")
    inc(PE.matmul(T.pss[:, 1:16], T.ones[:], T.ws[:, 1:16], False, True), "ps")
    need("v", "t1")
    inc(V.tensor_tensor(T.t2[:], T.t1[:], T.vv[:], A.mult), "t2")
    need("v", "dd")
    inc(V.tensor_tensor_scan(T.ft[:], T.d0[:], T.d1[:], 0.0, A.mult, A.add), "ft")
    need("v", "t2")
    inc(V.tensor_copy(T.po[:], T.t2[:]), "po")
    need("s", "po", "ft")
    inc(SC.activation(T.pm[:], T.ft[:].indirect(T.po[:]), AF.Copy), "pm")

    need("v", "ps")
    ts("su", T.su[:], T.pss[:, 0:16], 256.0, None, A.mult)
    ts("br", T.br[:], T.c16[:], pa, 1.0 / 256, A.add, A.mult)
    need("v", "su", "win")
    ts("b1", T.b1[:], T.wn[:].indirect(T.su[:]), T.cf[:, 3:4], None, A.mult)
    need("v", "br")
    inc(V.tensor_tensor(T.wt[:], T.wdt[:], T.br[:], A.add), "wt")
    need("v", "b1")
    ts("b2", T.b2[:], T.b1[:], 8, 255, A.logical_shift_right, A.bitwise_and)
    need("v", "wt")
    ts("wo", T.wo[:], T.wt[:], -1.0, 256.0, A.add, A.mult)
    need("v", "b2", "wo", "zh", "zc")
    inc(V.tensor_copy(T.zb[:, 0:2048].indirect(T.wo[:]), T.b2[:]), "zs")
    need("p", "zs", "pm")
    for v in range(8):
        ins = PE.matmul(T.psd[:, 0:B], T.pm[:, 128 * v:128 * v + 128], T.zb[:, B * v:B * v + B], v == 0, v == 7)
    inc(ins, "pd")
    inc(V.memset(T.two[:], 2.0), "two")
    inc(V.memset(T.dicw[:], 0.0), "dz")
    need("y", "dz")
    inc(SY.dma_start(T.dicw[0::16, :], T.dic[:]), "dic", 16)
    inc(V.tensor_copy(T.wu[:], T.wdt[:]), "pw")
    ts("sl", T.sl[:], T.sc[:, 7::8], 256.0, None, A.mult)
    need("v", "two")
    inc(V.tensor_tensor_scan(T.pw[:], T.two[:], T.two[:], 0.5, A.mult, A.max), "pw")
    need("v", "pd")
    inc(V.tensor_copy(T.u1[:], T.psd[:, 0:B]), "u1")
    need("v", "u1")
    ts("u2", T.u2[:], T.u1[:], 65535, None, A.bitwise_and)
    need("v", "u2", "pw")
    inc(V.tensor_tensor(T.u3[:], T.pw[:].indirect(T.wu[:]), T.u2[:], A.mult), "u3")
    need("v", "u3")
    ts("tab", T.tab[:], T.u3[:], 17, None, A.logical_shift_right)

    need("v", "tab", "rqx")
    inc(V.tensor_copy(T.sx[:], T.tab[:].indirect(T.rqi[:, 0:8])), "sx")
    need("g", "sx")
    tr = [RemoteDMATransfer(dst_ids=[_dst(topo, h, core)], dma_engine_mask=_mask(me["e_r2"][k]),
                            remote_sem=T.sem.h2, src=T.sx[:, 64 * k:64 * k + 64], dst=T.rl2[:])
          for k, h in enumerate(me["relays"])]
    g.remote_dma_fused(tr, local_sem=T.sem.loc)
    nloc += sum(len(e) for e in me["e_r2"])
    need("v", "rqd")
    inc(V.tensor_copy(T.sd[:], T.tab[:].indirect(T.rqi[:, 8:14])), "sd")
    need("g", "sd")
    tr = []
    for i, q in enumerate(me["direct"]):
        tr.append(RemoteDMATransfer(dst_ids=[_dst(topo, cores[q], core)], dma_engine_mask=_mask(me["e_dir"][i]),
                                    remote_sem=T.sem.rsd, src=T.sd[:, 32 * i:32 * i + NB],
                                    dst=T.zb[:, RSP + 32 * rank:RSP + 32 * rank + NB]))
    g.remote_dma_fused(tr, local_sem=T.sem.loc)
    nloc += sum(len(e) for e in me["e_dir"])
    need("v", "rqo")
    inc(V.tensor_copy(T.zb[:, RSP + 32 * rank:RSP + 32 * rank + 32],
                      T.tab[:].indirect(T.rqo[:, 2 * rank:2 * rank + 2])), "own")

    need("v", "own", "sl", "dic", "rsd", "rsx")
    inc(V.tensor_copy(T.cu[:], T.zb[:, RSP:RSP + 256].indirect(T.sl[:])), "cu")
    need("s", "dic", "cu")
    inc(SC.activation(T.yy[:, 1024:2048], T.dicw[:].indirect(T.cu[:, 64:128]), AF.Copy), "y1")
    need("v", "cu")
    inc(V.tensor_copy(T.yy[:, 0:1024], T.dicw[:].indirect(T.cu[:, 0:64])), "y0")
    need("s", "y1")
    inc(SC.dma_start(T.y[:, 1024:2048], T.yy[0::16, 1024:2048]), "st1", 16)
    need("y", "y0")
    inc(SY.dma_start(T.y[:, 0:1024], T.yy[0::16, 0:1024]), "st0", 16)
    need("s", "st1")
    need("y", "st0")
    g.wait_ge(T.sem.loc, nloc)
